import numpy as np
import ml_dtypes


def mxq(x, axis, fmt="e4m3"):
    dtype, down = {"e4m3": (ml_dtypes.float8_e4m3fn, 7), "e5m2": (ml_dtypes.float8_e5m2, 14)}[fmt]
    v = np.moveaxis(np.asarray(x, np.float32).astype(ml_dtypes.bfloat16).astype(np.float64), axis, -1)
    blocks = v.reshape(v.shape[:-1] + (-1, 32))
    amax = np.abs(blocks).max(-1, keepdims=True)
    byte = np.maximum(np.where(amax > 0, np.frexp(amax)[1] - 1 + 127, 0) - down, 1)
    scale = np.exp2(byte - 127.0)
    codes = (blocks / scale).astype(np.float32).astype(dtype).astype(np.float64)
    return np.moveaxis((codes * scale).reshape(v.shape), -1, axis)


WIDE = False


def mx_kscale(k):
    if not WIDE:
        return np.ones(k)
    levels = np.array([24, -24, 12, -12, 0])
    if k % 512:
        return np.exp2(np.random.permutation(np.resize(levels, k // 32))).repeat(32)
    a = np.empty((k // 512, 16))
    for p in range(k // 512):
        a[p, :8] = np.random.permutation(np.resize(levels, 8))
        for g in range(8):
            far = levels[np.abs(levels - a[p, g]) >= 10]
            a[p, g + 8] = far[np.random.randint(len(far))]
    return np.exp2(a.ravel()).repeat(32)


def f64(x):
    return np.asarray(x).astype(np.float64)


def striped(idx):
    return np.tile(idx.reshape(-1, 16).T, (8, 1)).astype(np.uint16)


def unstriped(offs):
    return offs[:16].T.reshape(-1).astype(np.int64)


E2M1 = np.array([0.0, 0.5, 1.0, 1.5, 2.0, 3.0, 4.0, 6.0, -0.0, -0.5, -1.0, -1.5, -2.0, -3.0, -4.0, -6.0])


def pack_weight(w, fmt):
    k, n = w.shape
    w = f64(np.asarray(w, np.float32).astype(ml_dtypes.bfloat16)).reshape(k // 32, 32, n)
    amax = np.abs(w).max(1)
    if fmt == "e4m3":
        byte = np.frexp(amax)[1] - 1 + 127 - 7
    else:
        mant, ex = np.frexp(amax / 6.0)
        byte = np.where(mant > 0.5, ex, ex - 1) + 127
    byte = np.clip(np.where(amax > 0, byte, 1), 1, 254)
    scaled = (w * np.exp2(127.0 - byte)[:, None, :]).reshape(k, n).astype(np.float32)
    by_word = np.ascontiguousarray(scaled.reshape(k // 512, 128, 4, n).transpose(0, 1, 3, 2))
    if fmt == "e4m3":
        words = by_word.astype(ml_dtypes.float8_e4m3fn).view(np.uint8)
    else:
        c = by_word.astype(ml_dtypes.float4_e2m1fn).view(np.uint8) & 0xF
        words = (c[..., 0::2] | (c[..., 1::2] << 4)).reshape(k // 512, 128, 2 * n)
    return np.ascontiguousarray(words), np.ascontiguousarray(byte.astype(np.uint8).reshape(k // 512, 16, n))


def unpack_weight(words, scales, fmt):
    g, _, n = scales.shape
    words = np.ascontiguousarray(words).reshape(g, 128, n, -1)
    if fmt == "e4m3":
        vals = words.view(ml_dtypes.float8_e4m3fn).astype(np.float64)
    else:
        nib = np.empty((g, 128, n, 4), np.uint8)
        nib[..., 0::2] = words & 0xF
        nib[..., 1::2] = words >> 4
        vals = E2M1[nib]
    vals = vals * np.repeat(np.exp2(scales.astype(np.float64) - 127.0), 8, axis=1)[..., None]
    return vals.transpose(0, 1, 3, 2).reshape(g * 512, n)


def silu(f):
    return f / (1.0 + np.exp(-np.maximum(f, -700.0)))


K, M, N, J, T = 1024, 512, 256, 1024, 4096


def setup_inputs():
    n = np.random.standard_normal
    s = mx_kscale(K)[:, None]
    u = mx_kscale(J)[:, None]
    p_tab = pack_weight(0.5 * n((K, T)) / np.sqrt(K) / s, "e4m3")
    return {
        "x": (n((K, M)) * s).astype(np.float32),
        "tab_words": p_tab[0],
        "tab_scales": p_tab[1],
        "cw": (np.random.uniform(0.5, 2.0, J) * u[:, 0]).astype(np.float32),
        "cb": (0.3 * n(J)).astype(np.float32),
        "al": (n((J, N)) / np.sqrt(J) / u).astype(np.float32),
        "b": (0.3 * n(N)).astype(np.float32),
        "offs": striped(np.random.permutation(T)[:J]),
    }


def reference(x, tab_words, tab_scales, cw, cb, al, b, offs):
    idx = unstriped(offs)
    x_ = mxq(f64(x), 0, "e4m3")
    tab_ = unpack_weight(tab_words, tab_scales, "e4m3")[:, idx]
    d = tab_.T @ x_
    h = f64(cw)[:, None] * np.maximum(d + f64(cb)[:, None], 0.0)
    h_ = mxq(h, 0, "e4m3")
    al_ = mxq(f64(al), 0, "e4m3")
    y = al_.T @ h_
    return silu(y + f64(b)[:, None])

@@ -1,0 +1,294 @@
+from contextlib import ExitStack
+
+import concourse.mybir as mybir
+
+K, M, N, J, T = 1024, 512, 256, 1024, 4096
+FLOPS = 2 * K * J * M + 2 * J * N * M
+
+F32 = mybir.dt.float32
+BF16 = mybir.dt.bfloat16
+I32 = mybir.dt.int32
+U32 = mybir.dt.uint32
+U16 = mybir.dt.uint16
+U8 = mybir.dt.uint8
+FP8X4 = mybir.dt.float8_e4m3fn_x4
+ACT = mybir.ActivationFunctionType
+ALU = mybir.AluOpType
+
+P = 128
+PACK = 4
+PASS = P * PACK
+W = 256
+CHUNKS = M // W
+KP = K // PASS
+JP = J // PASS
+NT = N // P
+RUN = 4
+
+
+def weave_views(woven, planes):
+    return (
+        woven.rearrange("p (c i) t -> p c t i", i=RUN),
+        planes.rearrange("p t (c i) -> p c t i", i=RUN),
+    )
+
+
+def weave_vector(nc, woven, planes):
+    dst, src = weave_views(woven, planes)
+    nc.vector.tensor_copy(out=dst, in_=src)
+
+
+def weave_scalar(nc, woven, planes):
+    dst, src = weave_views(woven, planes)
+    nc.scalar.copy(out=dst, in_=src)
+
+
+def quantize(nc, pool, name, woven):
+    width = woven.shape[1]
+    codes = pool.tile([P, width], U32, name=name + "_codes", align_bytes=64)
+    scales = pool.tile([P, width], U8, name=name + "_scales", align_bytes=64)
+    nc.vector.quantize_mx(
+        out=codes[:].bitcast(FP8X4),
+        scales=scales[:],
+        in_=woven[:].rearrange("p w t -> p (w t)"),
+    )
+    return codes, scales
+
+
+def tile_list_kernl_arc_silu_kernel(
+    tc, x, tab_words, tab_scales, cw, cb, al, b, offs, out
+):
+    nc = tc.nc
+    with ExitStack() as ctx:
+        keep = ctx.enter_context(tc.tile_pool(name="keep", bufs=1))
+        psum_d = ctx.enter_context(tc.psum_pool(name="psum_d", bufs=5))
+        psum_y = ctx.enter_context(tc.psum_pool(name="psum_y", bufs=3))
+
+        offsets = keep.tile([P, J // 16], U16, name="offsets")
+
+        warm = keep.tile([P, 8], F32, name="warm")
+        nc.gpsimd.memset(warm[:], 0.0)
+        warm_out = keep.tile([P, 8], F32, name="warm_out")
+        nc.scalar.activation(out=warm_out[:], in_=warm[:], func=ACT.Silu)
+
+        cw_t = keep.tile([P, JP, PACK], F32, name="cw_t")
+        cb_t = keep.tile([P, JP, PACK], F32, name="cb_t")
+        b_t = keep.tile([P, NT], F32, name="b_t")
+        scale_win = keep.tile([P, T], U8, name="scale_win", align_bytes=64)
+        nc.vector.memset(scale_win[:].bitcast(I32), 0)
+
+        al_raw = [keep.tile([P, PACK, N], F32, name="al_raw%d" % g) for g in range(JP)]
+        word_win = [
+            keep.tile([P, T], U32, name="word_win%d" % a, align_bytes=64) for a in range(KP)
+        ]
+
+        def load_al(g):
+            nc.sync.dma_start(
+                out=al_raw[g][:],
+                in_=al[g * PASS : (g + 1) * PASS, :].rearrange("(p t) n -> p t n", t=PACK),
+            )
+
+        def load_words(a):
+            nc.sync.dma_start(
+                out=word_win[a][:].bitcast(I32),
+                in_=tab_words[a].rearrange("p t i -> p (t i)").bitcast(I32),
+            )
+
+        nc.sync.dma_start(out=cw_t[:], in_=cw.rearrange("(g p t) -> p g t", p=P, t=PACK))
+        nc.sync.dma_start(offsets[:], offs)
+        load_al(0)
+        for q in range(4):
+            nc.sync.dma_start(
+                out=scale_win[32 * q : 32 * q + 4 * KP, :].bitcast(I32),
+                in_=tab_scales[:, 4 * q : 4 * q + 4, :].bitcast(I32),
+            )
+        load_words(0)
+        load_al(1)
+        nc.sync.dma_start(out=cb_t[:], in_=cb.rearrange("(g p t) -> p g t", p=P, t=PACK))
+        load_words(1)
+        x_raw = {}
+        for c in range(CHUNKS):
+            for a in range(KP):
+                raw = keep.tile([P, PACK, W], F32, name="x_raw%d%d" % (c, a))
+                nc.sync.dma_start(
+                    out=raw[:],
+                    in_=x[a * PASS : (a + 1) * PASS, c * W : (c + 1) * W].rearrange(
+                        "(p t) m -> p t m", t=PACK
+                    ),
+                )
+                x_raw[c, a] = raw
+        with nc.allow_non_contiguous_dma(reason="one bias value a partition"):
+            nc.sync.dma_start(out=b_t[:], in_=b.rearrange("(u p) -> p u", p=P))
+
+        sign = keep.tile([P, JP, PACK], F32, name="sign")
+        half = keep.tile([P, JP, PACK], F32, name="half")
+        gain = keep.tile([P, JP, PACK], F32, name="gain")
+        shift = keep.tile([P, JP, PACK], F32, name="shift")
+        nc.gpsimd.tensor_scalar(
+            out=half[:], in0=cw_t[:], scalar1=0.0, scalar2=2.0, op0=ALU.is_ge, op1=ALU.mult
+        )
+        nc.gpsimd.tensor_scalar(
+            out=sign[:], in0=half[:], scalar1=-1.0, scalar2=None, op0=ALU.add
+        )
+        nc.gpsimd.tensor_tensor(out=gain[:], in0=cw_t[:], in1=sign[:], op=ALU.mult)
+        nc.gpsimd.tensor_tensor(out=shift[:], in0=gain[:], in1=cb_t[:], op=ALU.mult)
+
+        al_woven = []
+        for g in range(JP):
+            signed = keep.tile([P, PACK, N], BF16, name="al_signed%d" % g)
+            for t in range(PACK):
+                nc.scalar.activation(
+                    out=signed[:, t, :],
+                    in_=al_raw[g][:, t, :],
+                    func=ACT.Copy,
+                    scale=sign[:, g, t : t + 1],
+                )
+            woven = keep.tile([P, N, PACK], BF16, name="al_woven%d" % g, align_bytes=64)
+            weave_scalar(nc, woven[:], signed[:])
+            al_woven.append(woven)
+
+        scale_picked = keep.tile([P, J], U8, name="scale_picked", align_bytes=64)
+        nc.vector.tensor_copy(scale_picked[:], scale_win[:].indirect(offsets[:]))
+        v_scales = keep.tile([P, J], U8, name="v_scales", align_bytes=64)
+        nc.vector.tensor_copy(
+            out=v_scales[:].rearrange("p (g t m) -> p g t m", g=JP, t=PACK),
+            in_=scale_picked[:].rearrange("p (g m t) -> p g t m", g=JP, t=PACK),
+        )
+
+        v_codes = {}
+
+        def gather_words(a, g):
+            picked = keep.tile([P, PASS], U32, name="v_codes%d%d" % (a, g), align_bytes=64)
+            cols = PASS // 16
+            nc.vector.tensor_copy(
+                picked[:].rearrange("p (t m) -> p m t", t=PACK),
+                word_win[a][:].indirect(offsets[:, g * cols : (g + 1) * cols]),
+            )
+            v_codes[a, g] = picked
+
+        gather_words(0, 0)
+        gather_words(0, 1)
+        al_q = [quantize(nc, keep, "al%d" % g, al_woven[g]) for g in range(JP)]
+        gather_words(1, 0)
+        gather_words(1, 1)
+
+        x_woven = {}
+        x_q = {}
+        h_planes = {}
+        h_woven = {}
+        h_q = {}
+
+        def weave_x(c, a, weave):
+            woven = keep.tile([P, W, PACK], BF16, name="x_woven%d%d" % (c, a), align_bytes=64)
+            weave(nc, woven[:], x_raw[c, a][:])
+            x_woven[c, a] = woven
+
+        def quantize_x(c, a):
+            x_q[c, a] = quantize(nc, keep, "x%d%d" % (c, a), x_woven[c, a])
+
+        def first_product(c, g, shared):
+            banks = [psum_d.tile([P, 2, W], F32, name="d_bank") for u in range(2)]
+            for a in range(KP):
+                for t in range(PACK):
+                    cols = slice(t * P, (t + 1) * P)
+                    wide = slice(g * PASS + t * P, g * PASS + (t + 1) * P)
+                    nc.tensor.matmul_mx(
+                        out=banks[t // 2][:, t % 2, :],
+                        lhsT=v_codes[a, g][:, cols].bitcast(FP8X4),
+                        lhsT_scale=v_scales[4 * a : P, wide],
+                        rhs=x_q[c, a][0][:].bitcast(FP8X4),
+                        rhs_scale=x_q[c, a][1][:],
+                        start=(a == 0 and t % 2 == 0),
+                        stop=(a == KP - 1 and t % 2 == 1),
+                    )
+            planes = keep.tile(
+                [P, PACK, W], F32 if shared else BF16, name="h_planes%d%d" % (c, g)
+            )
+            for t in range(PACK):
+                if shared and t >= 2:
+                    nc.vector.tensor_scalar(
+                        out=planes[:, t, :],
+                        in0=banks[t // 2][:, t % 2, :],
+                        scalar1=gain[:, g, t : t + 1],
+                        scalar2=shift[:, g, t : t + 1],
+                        op0=ALU.mult,
+                        op1=ALU.add,
+                    )
+                else:
+                    nc.scalar.activation(
+                        out=planes[:, t, :],
+                        in_=banks[t // 2][:, t % 2, :],
+                        func=ACT.Relu,
+                        scale=gain[:, g, t : t + 1],
+                        bias=shift[:, g, t : t + 1],
+                    )
+            h_planes[c, g] = planes
+
+        def weave_h(c, g, lo, hi):
+            woven = keep.tile(
+                [P, hi - lo, PACK], BF16, name="h_woven%d%d_%d" % (c, g, lo), align_bytes=64
+            )
+            dst, src = weave_views(woven[:], h_planes[c, g][:, :, lo:hi])
+            nc.vector.tensor_scalar(
+                out=dst, in0=src, scalar1=0.0, scalar2=None, op0=ALU.max
+            )
+            h_woven[c, g, lo] = woven
+
+        def quantize_h(c, g, lo):
+            h_q[c, g, lo] = quantize(nc, keep, "h%d%d_%d" % (c, g, lo), h_woven[c, g, lo])
+
+        def second_product(c, lo, hi, firsts):
+            bank = psum_y.tile([P, NT, W], F32, name="y_bank")
+            for g in range(JP):
+                codes, scales = h_q[c, g, firsts[g]]
+                part = slice(lo - firsts[g], hi - firsts[g])
+                for u in range(NT):
+                    cols = slice(u * P, (u + 1) * P)
+                    nc.tensor.matmul_mx(
+                        out=bank[:, u, 0 : hi - lo],
+                        lhsT=al_q[g][0][:, cols].bitcast(FP8X4),
+                        lhsT_scale=al_q[g][1][:, cols],
+                        rhs=codes[:, part].bitcast(FP8X4),
+                        rhs_scale=scales[:, part],
+                        start=(g == 0 and u == 0),
+                        stop=(g == JP - 1 and u == NT - 1),
+                    )
+            result = keep.tile([P, NT, hi - lo], F32, name="result%d_%d" % (c, lo))
+            for u in range(NT):
+                nc.scalar.activation(
+                    out=result[:, u, :],
+                    in_=bank[:, u, 0 : hi - lo],
+                    func=ACT.Silu,
+                    bias=b_t[:, u : u + 1],
+                )
+            nc.sync.dma_start(
+                out=out[:, c * W + lo : c * W + hi].rearrange("(u p) m -> p u m", p=P),
+                in_=result[:],
+            )
+
+        half_w = W // 2
+        weave_x(0, 0, weave_scalar)
+        weave_x(0, 1, weave_vector)
+        quantize_x(0, 0)
+        quantize_x(0, 1)
+        weave_x(1, 0, weave_vector)
+        weave_x(1, 1, weave_vector)
+        quantize_x(1, 0)
+        quantize_x(1, 1)
+        first_product(0, 0, False)
+        first_product(0, 1, False)
+        first_product(1, 0, False)
+        weave_h(0, 0, 0, W)
+        weave_h(0, 1, 0, W)
+        quantize_h(0, 0, 0)
+        quantize_h(0, 1, 0)
+        first_product(1, 1, False)
+        weave_h(1, 0, 0, W)
+        second_product(0, 0, W, (0, 0))
+        weave_h(1, 1, 0, half_w)
+        quantize_h(1, 0, 0)
+        weave_h(1, 1, half_w, W)
+        quantize_h(1, 1, 0)
+        quantize_h(1, 1, half_w)
+        second_product(1, 0, half_w, (0, 0))
+        second_product(1, half_w, W, (0, half_w))

@@ -43,9 +43,9 @@ def weave_scalar(nc, woven, planes):
     nc.scalar.copy(out=dst, in_=src)
 
 
-def quantize(nc, pool, name, woven):
+def quantize(nc, pool, name, woven, tenant=None):
     width = woven.shape[1]
-    codes = pool.tile([P, width], U32, name=name + "_codes", align_bytes=64)
+    codes = pool.tile([P, width], U32, name=tenant or name + "_codes", align_bytes=64)
     scales = pool.tile([P, width], U8, name=name + "_scales", align_bytes=64)
     nc.vector.quantize_mx(
         out=codes[:].bitcast(FP8X4),
@@ -61,8 +61,7 @@ def tile_list_kernl_arc_silu_kernel(
     nc = tc.nc
     with ExitStack() as ctx:
         keep = ctx.enter_context(tc.tile_pool(name="keep", bufs=1))
-        psum_d = ctx.enter_context(tc.psum_pool(name="psum_d", bufs=5))
-        psum_y = ctx.enter_context(tc.psum_pool(name="psum_y", bufs=3))
+        psum = ctx.enter_context(tc.psum_pool(name="psum", bufs=8))
 
         offsets = keep.tile([P, J // 16], U16, name="offsets")
 
@@ -73,16 +72,16 @@ def tile_list_kernl_arc_silu_kernel(
 
         cw_t = keep.tile([P, JP, PACK], F32, name="cw_t")
         cb_t = keep.tile([P, JP, PACK], F32, name="cb_t")
-        b_t = keep.tile([P, NT], F32, name="b_t")
         scale_win = keep.tile([P, T], U8, name="scale_win", align_bytes=64)
         nc.vector.memset(scale_win[:].bitcast(I32), 0)
 
-        al_raw = [keep.tile([P, PACK, N], F32, name="al_raw%d" % g) for g in range(JP)]
+        al_raw = {}
         word_win = [
             keep.tile([P, T], U32, name="word_win%d" % a, align_bytes=64) for a in range(KP)
         ]
 
-        def load_al(g):
+        def load_al(g, tenant):
+            al_raw[g] = keep.tile([P, PACK, N], F32, name=tenant, align_bytes=64)
             nc.sync.dma_start(
                 out=al_raw[g][:],
                 in_=al[g * PASS : (g + 1) * PASS, :].rearrange("(p t) n -> p t n", t=PACK),
@@ -94,47 +93,49 @@ def tile_list_kernl_arc_silu_kernel(
                 in_=tab_words[a].rearrange("p t i -> p (t i)").bitcast(I32),
             )
 
+        x_raw = {}
+
+        def load_x(c, a, tenant):
+            raw = keep.tile([P, PACK, W], F32, name=tenant, align_bytes=64)
+            nc.sync.dma_start(
+                out=raw[:],
+                in_=x[a * PASS : (a + 1) * PASS, c * W : (c + 1) * W].rearrange(
+                    "(p t) m -> p t m", t=PACK
+                ),
+            )
+            x_raw[c, a] = raw
+
+        load_al(0, "al_raw0")
         nc.sync.dma_start(out=cw_t[:], in_=cw.rearrange("(g p t) -> p g t", p=P, t=PACK))
         nc.sync.dma_start(offsets[:], offs)
-        load_al(0)
-        for q in range(4):
+        for a in range(KP):
             nc.sync.dma_start(
-                out=scale_win[32 * q : 32 * q + 4 * KP, :].bitcast(I32),
-                in_=tab_scales[:, 4 * q : 4 * q + 4, :].bitcast(I32),
+                out=scale_win[4 * a : P : 8, :].bitcast(I32),
+                in_=tab_scales[a].bitcast(I32),
             )
-        load_words(0)
-        load_al(1)
         nc.sync.dma_start(out=cb_t[:], in_=cb.rearrange("(g p t) -> p g t", p=P, t=PACK))
+        load_words(0)
+        load_x(0, 0, "x_raw00")
         load_words(1)
-        x_raw = {}
-        for c in range(CHUNKS):
-            for a in range(KP):
-                raw = keep.tile([P, PACK, W], F32, name="x_raw%d%d" % (c, a))
-                nc.sync.dma_start(
-                    out=raw[:],
-                    in_=x[a * PASS : (a + 1) * PASS, c * W : (c + 1) * W].rearrange(
-                        "(p t) m -> p t m", t=PACK
-                    ),
-                )
-                x_raw[c, a] = raw
-        with nc.allow_non_contiguous_dma(reason="one bias value a partition"):
-            nc.sync.dma_start(out=b_t[:], in_=b.rearrange("(u p) -> p u", p=P))
 
         sign = keep.tile([P, JP, PACK], F32, name="sign")
         half = keep.tile([P, JP, PACK], F32, name="half")
         gain = keep.tile([P, JP, PACK], F32, name="gain")
         shift = keep.tile([P, JP, PACK], F32, name="shift")
-        nc.gpsimd.tensor_scalar(
+        nc.vector.tensor_scalar(
             out=half[:], in0=cw_t[:], scalar1=0.0, scalar2=2.0, op0=ALU.is_ge, op1=ALU.mult
         )
-        nc.gpsimd.tensor_scalar(
+        nc.vector.tensor_scalar(
             out=sign[:], in0=half[:], scalar1=-1.0, scalar2=None, op0=ALU.add
         )
-        nc.gpsimd.tensor_tensor(out=gain[:], in0=cw_t[:], in1=sign[:], op=ALU.mult)
-        nc.gpsimd.tensor_tensor(out=shift[:], in0=gain[:], in1=cb_t[:], op=ALU.mult)
+        nc.vector.tensor_tensor(out=gain[:], in0=cw_t[:], in1=sign[:], op=ALU.mult)
+        nc.vector.tensor_tensor(out=shift[:], in0=gain[:], in1=cb_t[:], op=ALU.mult)
 
-        al_woven = []
-        for g in range(JP):
+        al_woven = {}
+
+        al_signed = {}
+
+        def sign_al(g):
             signed = keep.tile([P, PACK, N], BF16, name="al_signed%d" % g)
             for t in range(PACK):
                 nc.scalar.activation(
@@ -143,9 +144,15 @@ def tile_list_kernl_arc_silu_kernel(
                     func=ACT.Copy,
                     scale=sign[:, g, t : t + 1],
                 )
-            woven = keep.tile([P, N, PACK], BF16, name="al_woven%d" % g, align_bytes=64)
-            weave_scalar(nc, woven[:], signed[:])
-            al_woven.append(woven)
+            al_signed[g] = signed
+
+        def weave_al(g, tenant):
+            woven = keep.tile([P, N, PACK], BF16, name=tenant, align_bytes=64)
+            weave_scalar(nc, woven[:], al_signed[g][:])
+            al_woven[g] = woven
+
+        sign_al(0)
+        weave_al(0, "al_woven0")
 
         scale_picked = keep.tile([P, J], U8, name="scale_picked", align_bytes=64)
         nc.vector.tensor_copy(scale_picked[:], scale_win[:].indirect(offsets[:]))
@@ -154,6 +161,15 @@ def tile_list_kernl_arc_silu_kernel(
             out=v_scales[:].rearrange("p (g t m) -> p g t m", g=JP, t=PACK),
             in_=scale_picked[:].rearrange("p (g m t) -> p g t m", g=JP, t=PACK),
         )
+        last = 32 * 3 + 4 * (KP - 1)
+        for i in range(1, 4):
+            nc.sync.dma_start(
+                out=v_scales[i : last + i + 1 : 4, :].bitcast(I32),
+                in_=v_scales[8 * i : last + 8 * i + 1 : 4, :].bitcast(I32),
+            )
+
+        load_al(1, "scale_picked")
+
 
         v_codes = {}
 
@@ -168,9 +184,9 @@ def tile_list_kernl_arc_silu_kernel(
 
         gather_words(0, 0)
         gather_words(0, 1)
-        al_q = [quantize(nc, keep, "al%d" % g, al_woven[g]) for g in range(JP)]
-        gather_words(1, 0)
-        gather_words(1, 1)
+        al_q = {0: quantize(nc, keep, "al0", al_woven[0])}
+        load_x(0, 1, "al_woven0")
+        load_x(1, 0, "word_win0")
 
         x_woven = {}
         x_q = {}
@@ -186,59 +202,49 @@ def tile_list_kernl_arc_silu_kernel(
         def quantize_x(c, a):
             x_q[c, a] = quantize(nc, keep, "x%d%d" % (c, a), x_woven[c, a])
 
-        def first_product(c, g, shared):
-            banks = [psum_d.tile([P, 2, W], F32, name="d_bank") for u in range(2)]
-            for a in range(KP):
-                for t in range(PACK):
-                    cols = slice(t * P, (t + 1) * P)
-                    wide = slice(g * PASS + t * P, g * PASS + (t + 1) * P)
-                    nc.tensor.matmul_mx(
-                        out=banks[t // 2][:, t % 2, :],
-                        lhsT=v_codes[a, g][:, cols].bitcast(FP8X4),
-                        lhsT_scale=v_scales[4 * a : P, wide],
-                        rhs=x_q[c, a][0][:].bitcast(FP8X4),
-                        rhs_scale=x_q[c, a][1][:],
-                        start=(a == 0 and t % 2 == 0),
-                        stop=(a == KP - 1 and t % 2 == 1),
-                    )
-            planes = keep.tile(
-                [P, PACK, W], F32 if shared else BF16, name="h_planes%d%d" % (c, g)
-            )
-            for t in range(PACK):
-                if shared and t >= 2:
-                    nc.vector.tensor_scalar(
-                        out=planes[:, t, :],
-                        in0=banks[t // 2][:, t % 2, :],
-                        scalar1=gain[:, g, t : t + 1],
-                        scalar2=shift[:, g, t : t + 1],
-                        op0=ALU.mult,
-                        op1=ALU.add,
-                    )
-                else:
-                    nc.scalar.activation(
-                        out=planes[:, t, :],
-                        in_=banks[t // 2][:, t % 2, :],
-                        func=ACT.Relu,
-                        scale=gain[:, g, t : t + 1],
-                        bias=shift[:, g, t : t + 1],
-                    )
-            h_planes[c, g] = planes
+        d_banks = {}
 
-        def weave_h(c, g, lo, hi):
+        def first_product(c, g, a):
+            if a == 0:
+                d_banks[c, g] = [psum.tile([P, 2, W], F32, name="bank") for u in range(2)]
+            for t in range(PACK):
+                cols = slice(t * P, (t + 1) * P)
+                wide = slice(g * PASS + t * P, g * PASS + (t + 1) * P)
+                nc.tensor.matmul_mx(
+                    out=d_banks[c, g][t // 2][:, t % 2, :],
+                    lhsT=v_codes[a, g][:, cols].bitcast(FP8X4),
+                    lhsT_scale=v_scales[4 * a : P, wide],
+                    rhs=x_q[c, a][0][:].bitcast(FP8X4),
+                    rhs_scale=x_q[c, a][1][:],
+                    start=(a == 0 and t % 2 == 0),
+                    stop=(a == KP - 1 and t % 2 == 1),
+                )
+
+        def activate(c, g, lo, hi):
+            banks = d_banks[c, g]
+            planes = keep.tile([P, PACK, hi - lo], BF16, name="h_planes%d%d_%d" % (c, g, lo))
+            for t in range(PACK):
+                nc.scalar.activation(
+                    out=planes[:, t, :],
+                    in_=banks[t // 2][:, t % 2, lo:hi],
+                    func=ACT.Relu,
+                    scale=gain[:, g, t : t + 1],
+                    bias=shift[:, g, t : t + 1],
+                )
+            h_planes[c, g, lo] = planes
+
+        def weave_h(c, g, lo, hi, weave):
             woven = keep.tile(
                 [P, hi - lo, PACK], BF16, name="h_woven%d%d_%d" % (c, g, lo), align_bytes=64
             )
-            dst, src = weave_views(woven[:], h_planes[c, g][:, :, lo:hi])
-            nc.vector.tensor_scalar(
-                out=dst, in0=src, scalar1=0.0, scalar2=None, op0=ALU.max
-            )
+            weave(nc, woven[:], h_planes[c, g, lo][:])
             h_woven[c, g, lo] = woven
 
         def quantize_h(c, g, lo):
             h_q[c, g, lo] = quantize(nc, keep, "h%d%d_%d" % (c, g, lo), h_woven[c, g, lo])
 
-        def second_product(c, lo, hi, firsts):
-            bank = psum_y.tile([P, NT, W], F32, name="y_bank")
+        def second_product(c, lo, hi, firsts, tenant):
+            bank = psum.tile([P, NT, W], F32, name="bank")
             for g in range(JP):
                 codes, scales = h_q[c, g, firsts[g]]
                 part = slice(lo - firsts[g], hi - firsts[g])
@@ -253,7 +259,7 @@ def tile_list_kernl_arc_silu_kernel(
                         start=(g == 0 and u == 0),
                         stop=(g == JP - 1 and u == NT - 1),
                     )
-            result = keep.tile([P, NT, hi - lo], F32, name="result%d_%d" % (c, lo))
+            result = keep.tile([P, NT, hi - lo], F32, name=tenant)
             for u in range(NT):
                 nc.scalar.activation(
                     out=result[:, u, :],
@@ -267,28 +273,43 @@ def tile_list_kernl_arc_silu_kernel(
             )
 
         half_w = W // 2
-        weave_x(0, 0, weave_scalar)
-        weave_x(0, 1, weave_vector)
+        weave_x(0, 0, weave_vector)
+        load_x(1, 1, "x_raw00")
         quantize_x(0, 0)
+        for g in range(JP):
+            first_product(0, g, 0)
+        gather_words(1, 0)
+        gather_words(1, 1)
+        b_t = keep.tile([P, NT], F32, name="word_win1", align_bytes=64)
+        with nc.allow_non_contiguous_dma(reason="one bias value a partition"):
+            nc.sync.dma_start(out=b_t[:], in_=b.rearrange("(u p) -> p u", p=P))
+        sign_al(1)
+        weave_al(1, "al_woven1")
+        weave_x(0, 1, weave_vector)
         quantize_x(0, 1)
-        weave_x(1, 0, weave_vector)
-        weave_x(1, 1, weave_vector)
-        quantize_x(1, 0)
-        quantize_x(1, 1)
-        first_product(0, 0, False)
-        first_product(0, 1, False)
-        first_product(1, 0, False)
-        weave_h(0, 0, 0, W)
-        weave_h(0, 1, 0, W)
+        for g in range(JP):
+            first_product(0, g, 1)
+        for a in range(KP):
+            weave_x(1, a, weave_vector)
+            quantize_x(1, a)
+            for g in range(JP):
+                first_product(1, g, a)
+        al_q[1] = quantize(nc, keep, "al1", al_woven[1], "x_woven11")
+        activate(0, 0, 0, W)
+        activate(0, 1, 0, W)
+        activate(1, 0, 0, W)
+        activate(1, 1, 0, half_w)
+        activate(1, 1, half_w, W)
+        weave_h(0, 0, 0, W, weave_vector)
+        weave_h(0, 1, 0, W, weave_vector)
         quantize_h(0, 0, 0)
         quantize_h(0, 1, 0)
-        first_product(1, 1, False)
-        weave_h(1, 0, 0, W)
-        second_product(0, 0, W, (0, 0))
-        weave_h(1, 1, 0, half_w)
+        weave_h(1, 0, 0, W, weave_vector)
+        second_product(0, 0, W, (0, 0), "shift")
+        weave_h(1, 1, 0, half_w, weave_vector)
         quantize_h(1, 0, 0)
-        weave_h(1, 1, half_w, W)
         quantize_h(1, 1, 0)
+        weave_h(1, 1, half_w, W, weave_vector)
         quantize_h(1, 1, half_w)
-        second_product(1, 0, half_w, (0, 0))
-        second_product(1, half_w, W, (0, half_w))
+        second_product(1, 0, half_w, (0, 0), "result_a")
+        second_product(1, half_w, W, (0, half_w), "result_b")

from contextlib import ExitStack

import concourse.mybir as mybir

K, M, N, J, T = 1024, 512, 256, 1024, 4096
FLOPS = 2 * K * J * M + 2 * J * N * M

F32 = mybir.dt.float32
BF16 = mybir.dt.bfloat16
I32 = mybir.dt.int32
U32 = mybir.dt.uint32
U16 = mybir.dt.uint16
U8 = mybir.dt.uint8
FP8X4 = mybir.dt.float8_e4m3fn_x4
ACT = mybir.ActivationFunctionType
ALU = mybir.AluOpType

P = 128
PACK = 4
PASS = P * PACK
W = 256
CHUNKS = M // W
KP = K // PASS
JP = J // PASS
NT = N // P
RUN = 4


def weave_views(woven, planes):
    return (
        woven.rearrange("p (c i) t -> p c t i", i=RUN),
        planes.rearrange("p t (c i) -> p c t i", i=RUN),
    )


def weave_vector(nc, woven, planes):
    dst, src = weave_views(woven, planes)
    nc.vector.tensor_copy(out=dst, in_=src)


def weave_scalar(nc, woven, planes):
    dst, src = weave_views(woven, planes)
    nc.scalar.copy(out=dst, in_=src)


def quantize(nc, pool, name, woven, tenant=None):
    width = woven.shape[1]
    codes = pool.tile([P, width], U32, name=tenant or name + "_codes", align_bytes=64)
    scales = pool.tile([P, width], U8, name=name + "_scales", align_bytes=64)
    nc.vector.quantize_mx(
        out=codes[:].bitcast(FP8X4),
        scales=scales[:],
        in_=woven[:].rearrange("p w t -> p (w t)"),
    )
    return codes, scales


def tile_list_kernl_arc_silu_kernel(
    tc, x, tab_words, tab_scales, cw, cb, al, b, offs, out
):
    nc = tc.nc
    with ExitStack() as ctx:
        keep = ctx.enter_context(tc.tile_pool(name="keep", bufs=1))
        psum = ctx.enter_context(tc.psum_pool(name="psum", bufs=8))

        offsets = keep.tile([P, J // 16], U16, name="offsets")

        warm = keep.tile([P, 8], F32, name="warm")
        nc.gpsimd.memset(warm[:], 0.0)
        warm_out = keep.tile([P, 8], F32, name="warm_out")
        nc.scalar.activation(out=warm_out[:], in_=warm[:], func=ACT.Silu)

        cw_t = keep.tile([P, JP, PACK], F32, name="cw_t")
        cb_t = keep.tile([P, JP, PACK], F32, name="cb_t")
        scale_win = keep.tile([P, T], U8, name="scale_win", align_bytes=64)
        nc.vector.memset(scale_win[:].bitcast(I32), 0)

        al_raw = {}
        word_win = [
            keep.tile([P, T], U32, name="word_win%d" % a, align_bytes=64) for a in range(KP)
        ]

        def load_al(g, tenant):
            al_raw[g] = keep.tile([P, PACK, N], F32, name=tenant, align_bytes=64)
            nc.sync.dma_start(
                out=al_raw[g][:],
                in_=al[g * PASS : (g + 1) * PASS, :].rearrange("(p t) n -> p t n", t=PACK),
            )

        def load_words(a):
            nc.sync.dma_start(
                out=word_win[a][:].bitcast(I32),
                in_=tab_words[a].rearrange("p t i -> p (t i)").bitcast(I32),
            )

        x_raw = {}

        def load_x(c, a, tenant):
            raw = keep.tile([P, PACK, W], F32, name=tenant, align_bytes=64)
            nc.sync.dma_start(
                out=raw[:],
                in_=x[a * PASS : (a + 1) * PASS, c * W : (c + 1) * W].rearrange(
                    "(p t) m -> p t m", t=PACK
                ),
            )
            x_raw[c, a] = raw

        load_al(0, "al_raw0")
        nc.sync.dma_start(out=cw_t[:], in_=cw.rearrange("(g p t) -> p g t", p=P, t=PACK))
        nc.sync.dma_start(offsets[:], offs)
        for a in range(KP):
            nc.sync.dma_start(
                out=scale_win[4 * a : P : 8, :].bitcast(I32),
                in_=tab_scales[a].bitcast(I32),
            )
        nc.sync.dma_start(out=cb_t[:], in_=cb.rearrange("(g p t) -> p g t", p=P, t=PACK))
        load_words(0)
        load_x(0, 0, "x_raw00")
        load_words(1)

        sign = keep.tile([P, JP, PACK], F32, name="sign")
        half = keep.tile([P, JP, PACK], F32, name="half")
        gain = keep.tile([P, JP, PACK], F32, name="gain")
        shift = keep.tile([P, JP, PACK], F32, name="shift")
        nc.vector.tensor_scalar(
            out=half[:], in0=cw_t[:], scalar1=0.0, scalar2=2.0, op0=ALU.is_ge, op1=ALU.mult
        )
        nc.vector.tensor_scalar(
            out=sign[:], in0=half[:], scalar1=-1.0, scalar2=None, op0=ALU.add
        )
        nc.vector.tensor_tensor(out=gain[:], in0=cw_t[:], in1=sign[:], op=ALU.mult)
        nc.vector.tensor_tensor(out=shift[:], in0=gain[:], in1=cb_t[:], op=ALU.mult)

        al_woven = {}

        al_signed = {}

        def sign_al(g):
            signed = keep.tile([P, PACK, N], BF16, name="al_signed%d" % g)
            for t in range(PACK):
                nc.scalar.activation(
                    out=signed[:, t, :],
                    in_=al_raw[g][:, t, :],
                    func=ACT.Copy,
                    scale=sign[:, g, t : t + 1],
                )
            al_signed[g] = signed

        def weave_al(g, tenant):
            woven = keep.tile([P, N, PACK], BF16, name=tenant, align_bytes=64)
            weave_scalar(nc, woven[:], al_signed[g][:])
            al_woven[g] = woven

        sign_al(0)
        weave_al(0, "al_woven0")

        scale_picked = keep.tile([P, J], U8, name="scale_picked", align_bytes=64)
        nc.vector.tensor_copy(scale_picked[:], scale_win[:].indirect(offsets[:]))
        v_scales = keep.tile([P, J], U8, name="v_scales", align_bytes=64)
        nc.vector.tensor_copy(
            out=v_scales[:].rearrange("p (g t m) -> p g t m", g=JP, t=PACK),
            in_=scale_picked[:].rearrange("p (g m t) -> p g t m", g=JP, t=PACK),
        )
        last = 32 * 3 + 4 * (KP - 1)
        for i in range(1, 4):
            nc.sync.dma_start(
                out=v_scales[i : last + i + 1 : 4, :].bitcast(I32),
                in_=v_scales[8 * i : last + 8 * i + 1 : 4, :].bitcast(I32),
            )

        load_al(1, "scale_picked")


        v_codes = {}

        def gather_words(a, g):
            picked = keep.tile([P, PASS], U32, name="v_codes%d%d" % (a, g), align_bytes=64)
            cols = PASS // 16
            nc.vector.tensor_copy(
                picked[:].rearrange("p (t m) -> p m t", t=PACK),
                word_win[a][:].indirect(offsets[:, g * cols : (g + 1) * cols]),
            )
            v_codes[a, g] = picked

        gather_words(0, 0)
        gather_words(0, 1)
        al_q = {0: quantize(nc, keep, "al0", al_woven[0])}
        load_x(0, 1, "al_woven0")
        load_x(1, 0, "word_win0")

        x_woven = {}
        x_q = {}
        h_planes = {}
        h_woven = {}
        h_q = {}

        def weave_x(c, a, weave):
            woven = keep.tile([P, W, PACK], BF16, name="x_woven%d%d" % (c, a), align_bytes=64)
            weave(nc, woven[:], x_raw[c, a][:])
            x_woven[c, a] = woven

        def quantize_x(c, a):
            x_q[c, a] = quantize(nc, keep, "x%d%d" % (c, a), x_woven[c, a])

        d_banks = {}

        def first_product(c, g, a):
            if a == 0:
                d_banks[c, g] = [psum.tile([P, 2, W], F32, name="bank") for u in range(2)]
            for t in range(PACK):
                cols = slice(t * P, (t + 1) * P)
                wide = slice(g * PASS + t * P, g * PASS + (t + 1) * P)
                nc.tensor.matmul_mx(
                    out=d_banks[c, g][t // 2][:, t % 2, :],
                    lhsT=v_codes[a, g][:, cols].bitcast(FP8X4),
                    lhsT_scale=v_scales[4 * a : P, wide],
                    rhs=x_q[c, a][0][:].bitcast(FP8X4),
                    rhs_scale=x_q[c, a][1][:],
                    start=(a == 0 and t % 2 == 0),
                    stop=(a == KP - 1 and t % 2 == 1),
                )

        def activate(c, g, lo, hi):
            banks = d_banks[c, g]
            planes = keep.tile([P, PACK, hi - lo], BF16, name="h_planes%d%d_%d" % (c, g, lo))
            for t in range(PACK):
                nc.scalar.activation(
                    out=planes[:, t, :],
                    in_=banks[t // 2][:, t % 2, lo:hi],
                    func=ACT.Relu,
                    scale=gain[:, g, t : t + 1],
                    bias=shift[:, g, t : t + 1],
                )
            h_planes[c, g, lo] = planes

        def weave_h(c, g, lo, hi, weave):
            woven = keep.tile(
                [P, hi - lo, PACK], BF16, name="h_woven%d%d_%d" % (c, g, lo), align_bytes=64
            )
            weave(nc, woven[:], h_planes[c, g, lo][:])
            h_woven[c, g, lo] = woven

        def quantize_h(c, g, lo):
            h_q[c, g, lo] = quantize(nc, keep, "h%d%d_%d" % (c, g, lo), h_woven[c, g, lo])

        def second_product(c, lo, hi, firsts, tenant):
            bank = psum.tile([P, NT, W], F32, name="bank")
            for g in range(JP):
                codes, scales = h_q[c, g, firsts[g]]
                part = slice(lo - firsts[g], hi - firsts[g])
                for u in range(NT):
                    cols = slice(u * P, (u + 1) * P)
                    nc.tensor.matmul_mx(
                        out=bank[:, u, 0 : hi - lo],
                        lhsT=al_q[g][0][:, cols].bitcast(FP8X4),
                        lhsT_scale=al_q[g][1][:, cols],
                        rhs=codes[:, part].bitcast(FP8X4),
                        rhs_scale=scales[:, part],
                        start=(g == 0 and u == 0),
                        stop=(g == JP - 1 and u == NT - 1),
                    )
            result = keep.tile([P, NT, hi - lo], F32, name=tenant)
            for u in range(NT):
                nc.scalar.activation(
                    out=result[:, u, :],
                    in_=bank[:, u, 0 : hi - lo],
                    func=ACT.Silu,
                    bias=b_t[:, u : u + 1],
                )
            nc.sync.dma_start(
                out=out[:, c * W + lo : c * W + hi].rearrange("(u p) m -> p u m", p=P),
                in_=result[:],
            )

        half_w = W // 2
        weave_x(0, 0, weave_vector)
        load_x(1, 1, "x_raw00")
        quantize_x(0, 0)
        for g in range(JP):
            first_product(0, g, 0)
        gather_words(1, 0)
        gather_words(1, 1)
        b_t = keep.tile([P, NT], F32, name="word_win1", align_bytes=64)
        with nc.allow_non_contiguous_dma(reason="one bias value a partition"):
            nc.sync.dma_start(out=b_t[:], in_=b.rearrange("(u p) -> p u", p=P))
        sign_al(1)
        weave_al(1, "al_woven1")
        weave_x(0, 1, weave_vector)
        quantize_x(0, 1)
        for g in range(JP):
            first_product(0, g, 1)
        for a in range(KP):
            weave_x(1, a, weave_vector)
            quantize_x(1, a)
            for g in range(JP):
                first_product(1, g, a)
        al_q[1] = quantize(nc, keep, "al1", al_woven[1], "x_woven11")
        activate(0, 0, 0, W)
        activate(0, 1, 0, W)
        activate(1, 0, 0, W)
        activate(1, 1, 0, half_w)
        activate(1, 1, half_w, W)
        weave_h(0, 0, 0, W, weave_vector)
        weave_h(0, 1, 0, W, weave_vector)
        quantize_h(0, 0, 0)
        quantize_h(0, 1, 0)
        weave_h(1, 0, 0, W, weave_vector)
        second_product(0, 0, W, (0, 0), "shift")
        weave_h(1, 1, 0, half_w, weave_vector)
        quantize_h(1, 0, 0)
        quantize_h(1, 1, 0)
        weave_h(1, 1, half_w, W, weave_vector)
        quantize_h(1, 1, half_w)
        second_product(1, 0, half_w, (0, 0), "result_a")
        second_product(1, half_w, W, (0, half_w), "result_b")
